import numpy as np
CORES = [50,51,178,179,306,307,434,435]
N = 8
WIDTHS = [120,30,0,240,120,480,30,0]
OFF = [0,120,150,150,390,510,990,1020]
C = 1020
def setup_inputs(rng):
    return {"x": rng.standard_normal((N, 128, C), dtype=np.float32)}
def reference(x):
    s = x.sum(axis=0, dtype=np.float64).astype(x.dtype)
    YW = max(WIDTHS)
    y = np.full((N, 128, YW), np.nan, x.dtype)
    for r in range(N):
        y[r][:, :WIDTHS[r]] = s[:, OFF[r]:OFF[r] + WIDTHS[r]]
    return {"y": y}

@@ -1,0 +1,194 @@
+from concourse.bass import DstId, RemoteDMATransfer
+from concourse.mybir import AluOpType
+
+CHIP = 6
+RA, RB = 2, 3
+
+UNITS = {
+    "q0": (120, 2, RB, 1), "q1": (120, 2, RB, 1), "q2": (120, 2, RB, 3), "q3": (120, 2, RB, 3),
+    "r4": (120, 2, RA, 1), "r0": (120, 0, RA, 3), "r3a": (120, 1, RB, 0), "r3b": (120, 1, RB, 0),
+    "r1": (30, 0, RB, 3), "r6": (30, 3, RA, 0),
+}
+STAGE = {"q0": 0, "q1": 1, "q2": 2, "q3": 3, "r3a": 4, "r3b": 5, "r4": 6, "r0": 7, "r1": 0, "r6": 1}
+PIECES = {
+    "Q01": (("q0", "q1"), 0, 64, 5), "Q23": (("q2", "q3"), 64, 128, 5), "R3": (("r3a", "r3b"), 0, 128, 3),
+    "R4": (("r4",), 0, 128, 4), "R0": (("r0",), 0, 128, 0), "R1": (("r1",), 0, 128, 1), "R6": (("r6",), 0, 128, 6),
+}
+PIECE_OF = {u: p for p in PIECES for u in PIECES[p][0]}
+SENDER = {
+    0: {"q0": 2, "q2": 3, "q1": 4, "r4": 1, "q3": 6, "r3a": 5, "r3b": 0, "r6": 7},
+    1: {"q0": 0, "q3": 1, "q2": 2, "q1": 4, "r4": 6, "r0": 5, "r6": 7, "r1": 7},
+    2: {"r3a": 0, "r3b": 4, "r0": 1, "r1": 5, "r6": 6},
+    3: {"r3a": 0, "q0": 1, "r1": 2, "r4": 3, "q2": 3, "r3b": 4, "q1": 5, "r0": 6, "q3": 7},
+}
+HELPER_ORDER = ("r6", "r1", "r3a", "r3b", "r0", "r4", "q0", "q1", "q2", "q3")
+LOADS = {
+    0: ("Q01", "Q23", "R4", "R3", "R1", "R0", "R6", "Y"),
+    1: ("R6", "R1", "Q23", "R0", "R3", "Q01", "R4", "Y"),
+    2: ("R1", "R0", "R6", "R3", "R4", "Q01", "Q23", "Y"),
+    3: ("R3", "Q01", "R4", "R1", "R6", "Q23", "R0", "Y"),
+}
+RANK_ACTS = {
+    (0, RA): [("S", ("q1", "q2", "q3", "r4"), (4, 4, 4, 4)), ("F", "q0"), ("S", ("r3a", "r3b"), (8, 8)),
+              ("S", ("r1", "r6"), (8, 8)), ("A", "pa"), ("A", "ea"), ("A", "la")],
+    (0, RB): [("S", ("q0", "q1", "q3", "r4"), (4, 4, 4, 4)), ("F", "q2"), ("S", ("r3a", "r3b", "r0"), (4, 4, 8)),
+              ("S", ("r6",), (16,)), ("A", "pa"), ("A", "ea"), ("A", "la")],
+    (1, RA): [("S", ("r6", "r1"), (8, 8)), ("S", ("q3", "r0", "r3a", "r3b"), (4, 4, 4, 4)),
+              ("S", ("q0", "q1", "r4"), (4, 4, 4)), ("F", "q2")],
+    (1, RB): [("S", ("r6", "r1"), (8, 8)), ("S", ("q2", "q3", "r0", "q0"), (4, 4, 4, 4)), ("S", ("q1", "r4"), (8, 8)),
+              ("A", "pa"), ("A", "ea"), ("A", "la")],
+    (2, RA): [("S", ("r1", "r6"), (8, 8)), ("S", ("r0", "r3a", "r3b"), (8, 4, 4)),
+              ("S", ("q0", "q1", "q2", "q3"), (4, 4, 4, 4)), ("A", "pa"), ("A", "ea"), ("A", "la")],
+    (2, RB): [("S", ("r1", "r6"), (8, 8)), ("S", ("r0", "r3a", "r3b", "r4"), (4, 4, 4, 4)),
+              ("A", "pa"), ("A", "ea"), ("A", "la")],
+    (3, RA): [("S", ("r3a", "r3b"), (8, 8)), ("S", ("q0", "q1", "r4", "q2"), (4, 4, 4, 4)), ("S", ("q3", "r0"), (8, 8)),
+              ("A", "pa"), ("F", "r1"), ("A", "ea"), ("A", "la")],
+    (3, RB): [("S", ("r3a", "r3b"), (8, 8)), ("S", ("q0", "q1", "q3", "r0"), (4, 4, 4, 4)), ("S", ("r1", "r6"), (8, 8)),
+              ("F", "r4"), ("F", "q2")],
+}
+OFFCHIP_ENGINES = 8
+
+
+def world(h, c):
+    return h * 128 + CHIP * 8 + c
+
+
+def build_plan():
+    acts = {}
+    for (h, c) in RANK_ACTS:
+        acts[(h, c)] = list(RANK_ACTS[(h, c)])
+    for h in SENDER:
+        for u in HELPER_ORDER:
+            c = SENDER[h].get(u)
+            if c is not None and c not in (RA, RB):
+                acts.setdefault((h, c), []).append(("F", u))
+    free = {}
+    group = {}
+    for key in acts:
+        rank_core = key[1] in (RA, RB)
+        free[key + (120,)] = 8 if rank_core else 0
+        free[key + (30,)] = 2 if rank_core else 0
+    for key in RANK_ACTS:
+        mine = sorted((u for u in UNITS if (UNITS[u][1], UNITS[u][2]) == key), key=lambda u: STAGE[u])
+        if not mine:
+            continue
+        w = UNITS[mine[0]][0]
+        group[key + ("pa",)] = (w, STAGE[mine[0]], mine)
+        for stage in ("ea", "la"):
+            group[key + (stage,)] = (w, free[key + (w,)], mine)
+            free[key + (w,)] += len(mine)
+    expect = {}
+    inputs = {}
+    route = {}
+    for key in sorted(acts):
+        h = key[0]
+        for i, act in enumerate(acts[key]):
+            todo = zip(act[1], act[2]) if act[0] == "S" else ([(act[1], OFFCHIP_ENGINES)] if act[0] == "F" else [])
+            for u, ne in todo:
+                w, dh, dc, via = UNITS[u]
+                if act[0] == "S" and dh != h:
+                    dst, sem = (h, SENDER[h][u]), "in_" + u
+                elif act[0] == "F" and h == (dh + 2) % 4:
+                    dst, sem = (via, SENDER[via][u]), "in_" + u
+                else:
+                    dst = (dh, dc)
+                    sem = "pa" if act[0] == "S" else ("la" if h == via else "ea")
+                if sem[:3] == "in_":
+                    slot = free[dst + (w,)]
+                    free[dst + (w,)] += 1
+                    inputs.setdefault(dst + (u,), []).append(slot)
+                else:
+                    gw, first, mine = group[dst + (sem,)]
+                    slot = first + mine.index(u)
+                expect[dst + (sem,)] = expect.get(dst + (sem,), 0) + ne
+                route[key + (i, u)] = (dst, slot, sem)
+    slots = {w: max(free[k] for k in free if k[2] == w) for w in (120, 30)}
+    return {"acts": acts, "group": group, "expect": expect, "inputs": inputs, "route": route, "slots": slots}
+
+
+PLAN = build_plan()
+
+SCRATCH = {
+    "d120": ("dram", [PLAN["slots"][120], 128, 120], "float32"),
+    "d30": ("dram", [PLAN["slots"][30], 128, 30], "float32"),
+}
+SEMAPHORES = (["in_" + u for u in sorted(UNITS)] + ["ld" + p for p in sorted(PIECES)]
+              + ["cp", "acc", "pa", "ea", "la", "snt"])
+
+
+def rank_program(g, core, T, topo):
+    key = (core // 128, core % 8)
+    if (core % 128) // 8 != CHIP or key not in PLAN["acts"]:
+        return
+    h, c = key
+    bufs = {120: T.d120, 30: T.d30}
+    rank = T.rank_of(core)
+    off, wid = T.tables["OFF"], T.tables["WIDTHS"]
+
+    if rank is not None:
+        queues, n = (g.sync, g.scalar), 0
+        for p in LOADS[h]:
+            if p == "Y":
+                if wid[rank]:
+                    queues[n % 2].dma_start(T.y[:, 0:wid[rank]], T.x[:, off[rank]:off[rank] + wid[rank]]).then_inc(T.sem.cp, 16)
+                    n += 1
+                continue
+            units, p0, p1, r = PIECES[p]
+            if r == rank:
+                continue
+            b, s = bufs[UNITS[units[0]][0]], STAGE[units[0]]
+            out = b[s] if len(units) == 1 else b[s:s + len(units)]
+            queues[n % 2].dma_start(out, T.x[p0:p1, off[r]:off[r] + wid[r]]).then_inc(T.sem["ld" + p], 16)
+            n += 1
+
+    loaded = set()
+
+    def need(u):
+        p = PIECE_OF[u]
+        if p not in loaded:
+            loaded.add(p)
+            g.wait_ge(T.sem["ld" + p], 16)
+
+    sent, added = 0, 0
+    for i, act in enumerate(PLAN["acts"][key]):
+        if act[0] == "S":
+            trs, bit = [], 0
+            for u, ne in zip(act[1], act[2]):
+                need(u)
+                dst, slot, sem = PLAN["route"][key + (i, u)]
+                rid, pid = topo.addr(world(dst[0], dst[1]), core)
+                b = bufs[UNITS[u][0]]
+                trs.append(RemoteDMATransfer(dst_ids=[DstId(rid=rid, pnc=pid)], dma_engine_mask=((1 << ne) - 1) << bit,
+                                             remote_sem=T.sem[sem], srcs=[b[STAGE[u]]], dsts=[b[slot]], alu_op=0))
+                bit += ne
+                sent += ne
+            g.remote_dma_fused(trs, local_sem=T.sem.snt)
+        elif act[0] == "F":
+            u = act[1]
+            b = bufs[UNITS[u][0]]
+            srcs = [b[s] for s in PLAN["inputs"][key + (u,)]]
+            if rank is not None:
+                need(u)
+                srcs.append(b[STAGE[u]])
+            g.wait_ge(T.sem["in_" + u], PLAN["expect"][key + ("in_" + u,)])
+            dst, slot, sem = PLAN["route"][key + (i, u)]
+            rid, pid = topo.addr(world(dst[0], dst[1]), core)
+            g.remote_dma_fused([RemoteDMATransfer(dst_ids=[DstId(rid=rid, pnc=pid)],
+                                                  dma_engine_mask=(1 << OFFCHIP_ENGINES) - 1, remote_sem=T.sem[sem],
+                                                  srcs=srcs, dsts=[b[slot]], alu_op=1)], local_sem=T.sem.snt)
+            sent += OFFCHIP_ENGINES
+        else:
+            stage = act[1]
+            w, first, mine = PLAN["group"][key + (stage,)]
+            g.wait_ge(T.sem[stage], PLAN["expect"][key + (stage,)])
+            if added:
+                g.wait_ge(T.sem.acc, added)
+            else:
+                g.wait_ge(T.sem.cp, 16)
+            src = bufs[w][first] if len(mine) == 1 else bufs[w][first:first + len(mine)]
+            g.dma_start(T.y[:, 0:wid[rank]], src, accum_op=AluOpType.add, max_dma_last_dim=8192).then_inc(T.sem.acc, 16)
+            added += 16
+    if added:
+        g.wait_ge(T.sem.acc, added)
+    if sent:
+        g.wait_ge(T.sem.snt, sent)

@@ -23,15 +23,15 @@ SENDER = {
 }
 HELPER_ORDER = ("r6", "r1", "r3a", "r3b", "r0", "r4", "q0", "q1", "q2", "q3")
 LOADS = {
-    0: ("Q01", "Q23", "R4", "R3", "R1", "R0", "R6", "Y"),
+    0: ("Q01", "Q23", "R4", "|", "R3", "R1", "R0", "R6", "Y"),
     1: ("R6", "R1", "Q23", "R0", "R3", "Q01", "R4", "Y"),
     2: ("R1", "R0", "R6", "R3", "R4", "Q01", "Q23", "Y"),
     3: ("R3", "Q01", "R4", "R1", "R6", "Q23", "R0", "Y"),
 }
 RANK_ACTS = {
-    (0, RA): [("S", ("q1", "q2", "q3", "r4"), (4, 4, 4, 4)), ("F", "q0"), ("S", ("r3a", "r3b"), (8, 8)),
+    (0, RA): [("S", ("q1", "q2", "q3", "r4"), (4, 4, 4, 4)), ("G",), ("F", "q0"), ("S", ("r3a", "r3b"), (8, 8)),
               ("S", ("r1", "r6"), (8, 8)), ("A", "pa"), ("A", "ea"), ("A", "la")],
-    (0, RB): [("S", ("q0", "q1", "q3", "r4"), (4, 4, 4, 4)), ("F", "q2"), ("S", ("r3a", "r3b", "r0"), (4, 4, 8)),
+    (0, RB): [("S", ("q0", "q1", "q3", "r4"), (4, 4, 4, 4)), ("G",), ("F", "q2"), ("S", ("r3a", "r3b", "r0"), (4, 4, 8)),
               ("S", ("r6",), (16,)), ("A", "pa"), ("A", "ea"), ("A", "la")],
     (1, RA): [("S", ("r6", "r1"), (8, 8)), ("S", ("q3", "r0", "r3a", "r3b"), (4, 4, 4, 4)),
               ("S", ("q0", "q1", "r4"), (4, 4, 4)), ("F", "q2")],
@@ -113,7 +113,7 @@ SCRATCH = {
     "d30": ("dram", [PLAN["slots"][30], 128, 30], "float32"),
 }
 SEMAPHORES = (["in_" + u for u in sorted(UNITS)] + ["ld" + p for p in sorted(PIECES)]
-              + ["cp", "acc", "pa", "ea", "la", "snt"])
+              + ["cp", "acc", "pa", "ea", "la", "snt", "go"])
 
 
 def rank_program(g, core, T, topo):
@@ -126,20 +126,28 @@ def rank_program(g, core, T, topo):
     off, wid = T.tables["OFF"], T.tables["WIDTHS"]
 
     if rank is not None:
-        queues, n = (g.sync, g.scalar), 0
+        queues, held, gate, n = (g.sync, g.scalar), [False, False], False, 0
         for p in LOADS[h]:
+            if p == "|":
+                gate = True
+                continue
             if p == "Y":
-                if wid[rank]:
-                    queues[n % 2].dma_start(T.y[:, 0:wid[rank]], T.x[:, off[rank]:off[rank] + wid[rank]]).then_inc(T.sem.cp, 16)
-                    n += 1
+                if not wid[rank]:
+                    continue
+            elif PIECES[p][3] == rank:
+                continue
+            q = queues[n % 2]
+            if gate and not held[n % 2]:
+                held[n % 2] = True
+                q.wait_ge(T.sem.go, 1)
+            n += 1
+            if p == "Y":
+                q.dma_start(T.y[:, 0:wid[rank]], T.x[:, off[rank]:off[rank] + wid[rank]]).then_inc(T.sem.cp, 16)
                 continue
             units, p0, p1, r = PIECES[p]
-            if r == rank:
-                continue
             b, s = bufs[UNITS[units[0]][0]], STAGE[units[0]]
             out = b[s] if len(units) == 1 else b[s:s + len(units)]
-            queues[n % 2].dma_start(out, T.x[p0:p1, off[r]:off[r] + wid[r]]).then_inc(T.sem["ld" + p], 16)
-            n += 1
+            q.dma_start(out, T.x[p0:p1, off[r]:off[r] + wid[r]]).then_inc(T.sem["ld" + p], 16)
 
     loaded = set()
 
@@ -151,7 +159,9 @@ def rank_program(g, core, T, topo):
 
     sent, added = 0, 0
     for i, act in enumerate(PLAN["acts"][key]):
-        if act[0] == "S":
+        if act[0] == "G":
+            g.sem_inc(T.sem.go, 1)
+        elif act[0] == "S":
             trs, bit = [], 0
             for u, ne in zip(act[1], act[2]):
                 need(u)

from concourse.bass import DstId, RemoteDMATransfer
from concourse.mybir import AluOpType

CHIP = 6
RA, RB = 2, 3

UNITS = {
    "q0": (120, 2, RB, 1), "q1": (120, 2, RB, 1), "q2": (120, 2, RB, 3), "q3": (120, 2, RB, 3),
    "r4": (120, 2, RA, 1), "r0": (120, 0, RA, 3), "r3a": (120, 1, RB, 0), "r3b": (120, 1, RB, 0),
    "r1": (30, 0, RB, 3), "r6": (30, 3, RA, 0),
}
STAGE = {"q0": 0, "q1": 1, "q2": 2, "q3": 3, "r3a": 4, "r3b": 5, "r4": 6, "r0": 7, "r1": 0, "r6": 1}
PIECES = {
    "Q01": (("q0", "q1"), 0, 64, 5), "Q23": (("q2", "q3"), 64, 128, 5), "R3": (("r3a", "r3b"), 0, 128, 3),
    "R4": (("r4",), 0, 128, 4), "R0": (("r0",), 0, 128, 0), "R1": (("r1",), 0, 128, 1), "R6": (("r6",), 0, 128, 6),
}
PIECE_OF = {u: p for p in PIECES for u in PIECES[p][0]}
SENDER = {
    0: {"q0": 2, "q2": 3, "q1": 4, "r4": 1, "q3": 6, "r3a": 5, "r3b": 0, "r6": 7},
    1: {"q0": 0, "q3": 1, "q2": 2, "q1": 4, "r4": 6, "r0": 5, "r6": 7, "r1": 7},
    2: {"r3a": 0, "r3b": 4, "r0": 1, "r1": 5, "r6": 6},
    3: {"r3a": 0, "q0": 1, "r1": 2, "r4": 3, "q2": 3, "r3b": 4, "q1": 5, "r0": 6, "q3": 7},
}
HELPER_ORDER = ("r6", "r1", "r3a", "r3b", "r0", "r4", "q0", "q1", "q2", "q3")
LOADS = {
    0: ("Q01", "Q23", "R4", "|", "R3", "R1", "R0", "R6", "Y"),
    1: ("R6", "R1", "Q23", "R0", "R3", "Q01", "R4", "Y"),
    2: ("R1", "R0", "R6", "R3", "R4", "Q01", "Q23", "Y"),
    3: ("R3", "Q01", "R4", "R1", "R6", "Q23", "R0", "Y"),
}
RANK_ACTS = {
    (0, RA): [("S", ("q1", "q2", "q3", "r4"), (4, 4, 4, 4)), ("G",), ("F", "q0"), ("S", ("r3a", "r3b"), (8, 8)),
              ("S", ("r1", "r6"), (8, 8)), ("A", "pa"), ("A", "ea"), ("A", "la")],
    (0, RB): [("S", ("q0", "q1", "q3", "r4"), (4, 4, 4, 4)), ("G",), ("F", "q2"), ("S", ("r3a", "r3b", "r0"), (4, 4, 8)),
              ("S", ("r6",), (16,)), ("A", "pa"), ("A", "ea"), ("A", "la")],
    (1, RA): [("S", ("r6", "r1"), (8, 8)), ("S", ("q3", "r0", "r3a", "r3b"), (4, 4, 4, 4)),
              ("S", ("q0", "q1", "r4"), (4, 4, 4)), ("F", "q2")],
    (1, RB): [("S", ("r6", "r1"), (8, 8)), ("S", ("q2", "q3", "r0", "q0"), (4, 4, 4, 4)), ("S", ("q1", "r4"), (8, 8)),
              ("A", "pa"), ("A", "ea"), ("A", "la")],
    (2, RA): [("S", ("r1", "r6"), (8, 8)), ("S", ("r0", "r3a", "r3b"), (8, 4, 4)),
              ("S", ("q0", "q1", "q2", "q3"), (4, 4, 4, 4)), ("A", "pa"), ("A", "ea"), ("A", "la")],
    (2, RB): [("S", ("r1", "r6"), (8, 8)), ("S", ("r0", "r3a", "r3b", "r4"), (4, 4, 4, 4)),
              ("A", "pa"), ("A", "ea"), ("A", "la")],
    (3, RA): [("S", ("r3a", "r3b"), (8, 8)), ("S", ("q0", "q1", "r4", "q2"), (4, 4, 4, 4)), ("S", ("q3", "r0"), (8, 8)),
              ("A", "pa"), ("F", "r1"), ("A", "ea"), ("A", "la")],
    (3, RB): [("S", ("r3a", "r3b"), (8, 8)), ("S", ("q0", "q1", "q3", "r0"), (4, 4, 4, 4)), ("S", ("r1", "r6"), (8, 8)),
              ("F", "r4"), ("F", "q2")],
}
OFFCHIP_ENGINES = 8


def world(h, c):
    return h * 128 + CHIP * 8 + c


def build_plan():
    acts = {}
    for (h, c) in RANK_ACTS:
        acts[(h, c)] = list(RANK_ACTS[(h, c)])
    for h in SENDER:
        for u in HELPER_ORDER:
            c = SENDER[h].get(u)
            if c is not None and c not in (RA, RB):
                acts.setdefault((h, c), []).append(("F", u))
    free = {}
    group = {}
    for key in acts:
        rank_core = key[1] in (RA, RB)
        free[key + (120,)] = 8 if rank_core else 0
        free[key + (30,)] = 2 if rank_core else 0
    for key in RANK_ACTS:
        mine = sorted((u for u in UNITS if (UNITS[u][1], UNITS[u][2]) == key), key=lambda u: STAGE[u])
        if not mine:
            continue
        w = UNITS[mine[0]][0]
        group[key + ("pa",)] = (w, STAGE[mine[0]], mine)
        for stage in ("ea", "la"):
            group[key + (stage,)] = (w, free[key + (w,)], mine)
            free[key + (w,)] += len(mine)
    expect = {}
    inputs = {}
    route = {}
    for key in sorted(acts):
        h = key[0]
        for i, act in enumerate(acts[key]):
            todo = zip(act[1], act[2]) if act[0] == "S" else ([(act[1], OFFCHIP_ENGINES)] if act[0] == "F" else [])
            for u, ne in todo:
                w, dh, dc, via = UNITS[u]
                if act[0] == "S" and dh != h:
                    dst, sem = (h, SENDER[h][u]), "in_" + u
                elif act[0] == "F" and h == (dh + 2) % 4:
                    dst, sem = (via, SENDER[via][u]), "in_" + u
                else:
                    dst = (dh, dc)
                    sem = "pa" if act[0] == "S" else ("la" if h == via else "ea")
                if sem[:3] == "in_":
                    slot = free[dst + (w,)]
                    free[dst + (w,)] += 1
                    inputs.setdefault(dst + (u,), []).append(slot)
                else:
                    gw, first, mine = group[dst + (sem,)]
                    slot = first + mine.index(u)
                expect[dst + (sem,)] = expect.get(dst + (sem,), 0) + ne
                route[key + (i, u)] = (dst, slot, sem)
    slots = {w: max(free[k] for k in free if k[2] == w) for w in (120, 30)}
    return {"acts": acts, "group": group, "expect": expect, "inputs": inputs, "route": route, "slots": slots}


PLAN = build_plan()

SCRATCH = {
    "d120": ("dram", [PLAN["slots"][120], 128, 120], "float32"),
    "d30": ("dram", [PLAN["slots"][30], 128, 30], "float32"),
}
SEMAPHORES = (["in_" + u for u in sorted(UNITS)] + ["ld" + p for p in sorted(PIECES)]
              + ["cp", "acc", "pa", "ea", "la", "snt", "go"])


def rank_program(g, core, T, topo):
    key = (core // 128, core % 8)
    if (core % 128) // 8 != CHIP or key not in PLAN["acts"]:
        return
    h, c = key
    bufs = {120: T.d120, 30: T.d30}
    rank = T.rank_of(core)
    off, wid = T.tables["OFF"], T.tables["WIDTHS"]

    if rank is not None:
        queues, held, gate, n = (g.sync, g.scalar), [False, False], False, 0
        for p in LOADS[h]:
            if p == "|":
                gate = True
                continue
            if p == "Y":
                if not wid[rank]:
                    continue
            elif PIECES[p][3] == rank:
                continue
            q = queues[n % 2]
            if gate and not held[n % 2]:
                held[n % 2] = True
                q.wait_ge(T.sem.go, 1)
            n += 1
            if p == "Y":
                q.dma_start(T.y[:, 0:wid[rank]], T.x[:, off[rank]:off[rank] + wid[rank]]).then_inc(T.sem.cp, 16)
                continue
            units, p0, p1, r = PIECES[p]
            b, s = bufs[UNITS[units[0]][0]], STAGE[units[0]]
            out = b[s] if len(units) == 1 else b[s:s + len(units)]
            q.dma_start(out, T.x[p0:p1, off[r]:off[r] + wid[r]]).then_inc(T.sem["ld" + p], 16)

    loaded = set()

    def need(u):
        p = PIECE_OF[u]
        if p not in loaded:
            loaded.add(p)
            g.wait_ge(T.sem["ld" + p], 16)

    sent, added = 0, 0
    for i, act in enumerate(PLAN["acts"][key]):
        if act[0] == "G":
            g.sem_inc(T.sem.go, 1)
        elif act[0] == "S":
            trs, bit = [], 0
            for u, ne in zip(act[1], act[2]):
                need(u)
                dst, slot, sem = PLAN["route"][key + (i, u)]
                rid, pid = topo.addr(world(dst[0], dst[1]), core)
                b = bufs[UNITS[u][0]]
                trs.append(RemoteDMATransfer(dst_ids=[DstId(rid=rid, pnc=pid)], dma_engine_mask=((1 << ne) - 1) << bit,
                                             remote_sem=T.sem[sem], srcs=[b[STAGE[u]]], dsts=[b[slot]], alu_op=0))
                bit += ne
                sent += ne
            g.remote_dma_fused(trs, local_sem=T.sem.snt)
        elif act[0] == "F":
            u = act[1]
            b = bufs[UNITS[u][0]]
            srcs = [b[s] for s in PLAN["inputs"][key + (u,)]]
            if rank is not None:
                need(u)
                srcs.append(b[STAGE[u]])
            g.wait_ge(T.sem["in_" + u], PLAN["expect"][key + ("in_" + u,)])
            dst, slot, sem = PLAN["route"][key + (i, u)]
            rid, pid = topo.addr(world(dst[0], dst[1]), core)
            g.remote_dma_fused([RemoteDMATransfer(dst_ids=[DstId(rid=rid, pnc=pid)],
                                                  dma_engine_mask=(1 << OFFCHIP_ENGINES) - 1, remote_sem=T.sem[sem],
                                                  srcs=srcs, dsts=[b[slot]], alu_op=1)], local_sem=T.sem.snt)
            sent += OFFCHIP_ENGINES
        else:
            stage = act[1]
            w, first, mine = PLAN["group"][key + (stage,)]
            g.wait_ge(T.sem[stage], PLAN["expect"][key + (stage,)])
            if added:
                g.wait_ge(T.sem.acc, added)
            else:
                g.wait_ge(T.sem.cp, 16)
            src = bufs[w][first] if len(mine) == 1 else bufs[w][first:first + len(mine)]
            g.dma_start(T.y[:, 0:wid[rank]], src, accum_op=AluOpType.add, max_dma_last_dim=8192).then_inc(T.sem.acc, 16)
            added += 16
    if added:
        g.wait_ge(T.sem.acc, added)
    if sent:
        g.wait_ge(T.sem.snt, sent)
